import numpy as np
import ml_dtypes


def mxq(x, axis, fmt="e4m3"):
    dtype, down = {"e4m3": (ml_dtypes.float8_e4m3fn, 7), "e5m2": (ml_dtypes.float8_e5m2, 14)}[fmt]
    v = np.moveaxis(np.asarray(x, np.float32).astype(ml_dtypes.bfloat16).astype(np.float64), axis, -1)
    blocks = v.reshape(v.shape[:-1] + (-1, 32))
    amax = np.abs(blocks).max(-1, keepdims=True)
    byte = np.maximum(np.where(amax > 0, np.frexp(amax)[1] - 1 + 127, 0) - down, 1)
    scale = np.exp2(byte - 127.0)
    codes = (blocks / scale).astype(np.float32).astype(dtype).astype(np.float64)
    return np.moveaxis((codes * scale).reshape(v.shape), -1, axis)


WIDE = False


def mx_kscale(k):
    if not WIDE:
        return np.ones(k)
    levels = np.array([10, -10, 5, -5, 0])
    if k % 512:
        return np.exp2(np.random.permutation(np.resize(levels, k // 32))).repeat(32)
    a = np.empty((k // 512, 16))
    for p in range(k // 512):
        a[p, :8] = np.random.permutation(np.resize(levels, 8))
        for g in range(8):
            far = levels[np.abs(levels - a[p, g]) >= 10]
            a[p, g + 8] = far[np.random.randint(len(far))]
    return np.exp2(a.ravel()).repeat(32)


def f64(x):
    return np.asarray(x).astype(np.float64)


def striped(idx):
    return np.tile(idx.reshape(-1, 16).T, (8, 1)).astype(np.uint16)


def unstriped(offs):
    return offs[:16].T.reshape(-1).astype(np.int64)


def striped8(idx):
    return np.concatenate([x.reshape(-1, 16).T for x in idx]).astype(np.uint16)


def runs(offs, k):
    lists = np.stack([offs[16 * r : 16 * r + 16].T.reshape(-1) for r in range(8)]).astype(np.int64)
    return lists[np.arange(k) % 512 // 64]


def pack_weight(w):
    k, n = w.shape
    w = f64(np.asarray(w, np.float32).astype(ml_dtypes.bfloat16)).reshape(k // 32, 32, n)
    amax = np.abs(w).max(1)
    byte = np.clip(np.where(amax > 0, np.frexp(amax)[1] - 1 + 127 - 7, 1), 1, 254)
    scaled = (w * np.exp2(127.0 - byte)[:, None, :]).reshape(k, n).astype(np.float32)
    words = np.ascontiguousarray(scaled.reshape(k // 512, 128, 4, n).transpose(0, 1, 3, 2)).astype(ml_dtypes.float8_e4m3fn).view(np.uint8)
    return words, np.ascontiguousarray(byte.astype(np.uint8).reshape(k // 512, 16, n))


def unpack_weight(words, scales):
    g, p, n, _ = words.shape
    vals = np.ascontiguousarray(words).view(ml_dtypes.float8_e4m3fn).astype(np.float64) * np.repeat(np.exp2(scales.astype(np.float64) - 127.0), 8, axis=1)[..., None]
    return vals.transpose(0, 1, 3, 2).reshape(g * 512, n)


E2M1 = np.array([0.0, 0.5, 1.0, 1.5, 2.0, 3.0, 4.0, 6.0, -0.0, -0.5, -1.0, -1.5, -2.0, -3.0, -4.0, -6.0])


def pack_fp4(w):
    k, n = w.shape
    w = f64(np.asarray(w, np.float32).astype(ml_dtypes.bfloat16)).reshape(k // 32, 32, n)
    amax = np.abs(w).max(1)
    mant, ex = np.frexp(amax / 6.0)
    byte = np.clip(np.where(amax > 0, np.where(mant > 0.5, ex, ex - 1) + 127, 1), 1, 254)
    scaled = (w * np.exp2(127.0 - byte)[:, None, :]).reshape(k, n).astype(np.float32)
    c = np.ascontiguousarray(scaled.reshape(k // 512, 128, 4, n).transpose(0, 1, 3, 2)).astype(ml_dtypes.float4_e2m1fn).view(np.uint8) & 0xF
    words = (c[..., 0::2] | (c[..., 1::2] << 4)).reshape(k // 512, 128, 2 * n)
    return np.ascontiguousarray(words), np.ascontiguousarray(byte.astype(np.uint8).reshape(k // 512, 16, n))


def unpack_fp4(words, scales):
    g, _, n = scales.shape
    words = np.ascontiguousarray(words).reshape(g, 128, n, 2)
    nib = np.empty((g, 128, n, 4), np.uint8)
    nib[..., 0::2] = words & 0xF
    nib[..., 1::2] = words >> 4
    vals = E2M1[nib] * np.repeat(np.exp2(scales.astype(np.float64) - 127.0), 8, axis=1)[..., None]
    return vals.transpose(0, 1, 3, 2).reshape(g * 512, n)


def sigmoid(v):
    return 1.0 / (1.0 + np.exp(-np.maximum(v, -700.0)))

def planes(y):
    n, m = y.shape
    v = y.astype(np.float32).astype(ml_dtypes.bfloat16).astype(np.float64).reshape(n // 32, 32, m)
    top = np.abs(v).max(1)
    byte = np.clip(np.where(top > 0, np.frexp(top)[1] - 1 + 127 - 7, 1), 1, 254)
    codes = (v * np.exp2(127.0 - byte)[:, None, :]).reshape(n, m).astype(np.float32).astype(ml_dtypes.float8_e4m3fn).view(np.uint8)
    words = codes.reshape(n // 512, 128, 4, m).transpose(0, 1, 3, 2)
    return np.ascontiguousarray(words), np.ascontiguousarray(byte.astype(np.uint8).reshape(n // 512, 16, m))


K, T, S, N, H, C = 512, 2048, 512, 512, 512, 512


def setup_inputs():
    n = np.random.standard_normal
    s = mx_kscale(K)[:, None]
    u = mx_kscale(S)
    packed_xT = pack_weight(n((K, T)) * s)
    packed_w1 = pack_fp4(n((K, H)) / np.sqrt(K) / s)
    packed_w2 = pack_fp4(n((H, N)) / np.sqrt(H) / u[:, None])
    return {
        "x_words": packed_xT[0],
        "x_scales": packed_xT[1],
        "w1_words": packed_w1[0],
        "w1_scales": packed_w1[1],
        "tau": np.random.uniform(0.3, 0.9, (H, 1)).astype(np.float32),
        "gn": (np.random.uniform(0.5, 1.5, (H, 1)) * u[:, None]).astype(np.float32),
        "w2_words": packed_w2[0],
        "w2_scales": packed_w2[1],
        "gs": (np.random.uniform(0.5, 1.5, (K, 1)) / s).astype(np.float32),
        "tau2": np.random.uniform(0.3, 0.9, (C, 1)).astype(np.float32),
        "offs": striped(np.random.permutation(T)[:S]),
        "n1": striped(np.random.permutation(S)),
        "n2": striped(np.random.permutation(S)),
        "n3": striped8(np.stack([np.random.permutation(S) for _ in range(8)])),
        "n4": striped8(np.stack([np.random.permutation(S) for _ in range(8)])),
        "cand": striped(np.random.permutation(T)[:C]),
        "n5": striped(np.random.permutation(S)),
        "n6": striped(np.random.permutation(S)),
    }


def reference(x_words, x_scales, w1_words, w1_scales, tau, gn, w2_words, w2_scales, gs, tau2, offs, n1, n2, n3, n4, cand, n5, n6):
    xq = unpack_weight(x_words, x_scales)[:, unstriped(offs)]
    y = unpack_fp4(w1_words, w1_scales).T @ xq
    top = y.max(axis=1, keepdims=True)
    ea = np.exp(f64(tau) * (y[:, unstriped(n1)] - top))
    ea2 = np.exp(f64(tau) * (y[:, unstriped(n2)] - top))
    z = f64(gn) * (y + np.log(ea + ea2 + 0.25))
    a = unpack_fp4(w2_words, w2_scales).T @ mxq(z, 0, "e4m3")
    x_cand = unpack_weight(x_words, x_scales)[:, unstriped(cand)]
    z2 = f64(gs) * (y * (sigmoid(y[np.arange(H)[:, None], runs(n3, H)] - (y[np.arange(H)[:, None], runs(n4, H)]))))
    b = 0.0625 * ((x_cand.T @ mxq(z2, 0, "e4m3")))
    top2 = b.max(axis=1, keepdims=True)
    ea3 = np.exp(f64(tau2) * (b[:, unstriped(n5)] - top2))
    out_0 = (0.5 * (a - a[:, unstriped(n6)])) / (ea3 + 0.25)
    return (out_0,) + planes(out_0)

@@ -1,0 +1,255 @@
+from contextlib import ExitStack
+
+import concourse.mybir as mybir
+
+K, T, S, N, H, C = 512, 2048, 512, 512, 512, 512
+FLOPS = 2 * K * H * S + 2 * H * N * S + 2 * K * C * S
+
+F32 = mybir.dt.float32
+BF16 = mybir.dt.bfloat16
+I32 = mybir.dt.int32
+U32 = mybir.dt.uint32
+U16 = mybir.dt.uint16
+U8 = mybir.dt.uint8
+FP8X4 = mybir.dt.float8_e4m3fn_x4
+FP4X4 = mybir.dt.float4_e2m1fn_x4
+ALU = mybir.AluOpType
+ACT = mybir.ActivationFunctionType
+
+P = 128
+PACK = 4
+HALF = S // 2
+OUT_CHUNKS = ((0, 256), (256, 128), (384, 128))
+
+
+def tile_picked_fkcdqxbelgcmp_none_po_kernel(
+    tc, x_words, x_scales, w1_words, w1_scales, tau, gn, w2_words, w2_scales, gs, tau2,
+    offs, n1, n2, n3, n4, cand, n5, n6, out_0, out_1, out_2,
+):
+    nc = tc.nc
+    with ExitStack() as ctx:
+        sb = ctx.enter_context(tc.tile_pool(name="sb", bufs=1))
+        psum = ctx.enter_context(tc.psum_pool(name="psum", bufs=1))
+
+        def load_list(name, dram):
+            tile = sb.tile([P, S // 16], U16, name=name)
+            nc.sync.dma_start(tile[:], dram)
+            return tile
+
+        def load_rows(name, dram):
+            tile = sb.tile([P, PACK], F32, name=name)
+            nc.sync.dma_start(tile[:], dram.rearrange("(p t) o -> p (t o)", t=PACK))
+            return tile
+
+        def load_scale_rows(tile, dram):
+            for q in range(4):
+                nc.sync.dma_start(tile[32 * q : 32 * q + 4, :].bitcast(I32), dram[0, 4 * q : 4 * q + 4, :].bitcast(I32))
+
+        def zeroed_bytes(name, width, engine):
+            tile = sb.tile([P, width], U8, name=name, align_bytes=64)
+            engine.memset(tile[:].bitcast(I32), 0)
+            return tile
+
+        def load_fp4_words(name, dram):
+            tile = sb.tile([P, 2 * H], U8, name=name, align_bytes=64)
+            nc.sync.dma_start(tile[:].bitcast(I32), dram[0].bitcast(I32))
+            return tile
+
+        def deal(engine_copy, name, src, dtype, view):
+            tile = sb.tile(list(src.shape), dtype, name=name, align_bytes=64)
+            engine_copy(
+                tile[:].bitcast(view).rearrange("p (t m) -> p t m", t=PACK),
+                src[:].bitcast(view).rearrange("p (m t) -> p t m", t=PACK),
+            )
+            return tile
+
+        def window(name, tag):
+            tile = sb.tile([P, 2 * S], F32, name=name, tag=tag)
+            nc.vector.memset(tile[:, S:], 0.0)
+            return tile
+
+        def planes(name, dtype=F32, tag=None):
+            return sb.tile([P, PACK, S], dtype, name=name, tag=tag or name, align_bytes=64)
+
+        def interleave(dst, src):
+            nc.vector.tensor_copy(
+                dst.rearrange("p (c i) t -> p c t i", i=4), src.rearrange("p t (c i) -> p c t i", i=4)
+            )
+
+        def quantise(name, planar):
+            woven = sb.tile([P, S, PACK], BF16, name=name + "_woven", align_bytes=64)
+            codes = sb.tile([P, S], U32, name=name + "_codes", align_bytes=64)
+            scales = sb.tile([P, S], U8, name=name + "_scales", align_bytes=64)
+            halves = [slice(h * HALF, (h + 1) * HALF) for h in range(2)]
+            for cols in halves:
+                interleave(woven[:, cols, :], planar[:, :, cols])
+            for cols in halves:
+                nc.vector.quantize_mx(
+                    out=codes[:, cols].bitcast(FP8X4), scales=scales[:, cols],
+                    in_=woven[:, cols, :].rearrange("p j t -> p (j t)"),
+                )
+            return codes, scales
+
+        def product(bank, lhs, lhs_scales, codes, scales, pieces):
+            width = S // pieces
+            for h in range(pieces):
+                cols = slice(h * width, (h + 1) * width)
+                nc.tensor.matmul_mx(
+                    out=bank[:, cols], lhsT=lhs, lhsT_scale=lhs_scales,
+                    rhs=codes[:, cols].bitcast(FP8X4), rhs_scale=scales[:, cols], start=True, stop=True,
+                )
+
+        def fp4_block(words, t):
+            return words[:, 2 * P * t : 2 * P * (t + 1)].bitcast(FP4X4)
+
+        xs_all = zeroed_bytes("xs_all", T, nc.vector)
+        w1s_raw = zeroed_bytes("w1s_raw", H, nc.gpsimd)
+        w2s_raw = zeroed_bytes("w2s_raw", N, nc.gpsimd)
+        offs_sb = load_list("offs_sb", offs)
+        w1w_raw = load_fp4_words("w1w_raw", w1_words)
+        load_scale_rows(xs_all, x_scales)
+        xw_all = sb.tile([P, T], I32, name="xw_all", align_bytes=64)
+        nc.sync.dma_start(xw_all[:], x_words[0].rearrange("p n t -> p (n t)").bitcast(I32))
+        load_scale_rows(w1s_raw, w1_scales)
+        n4_sb = load_list("n4_sb", n4)
+        n3_sb = load_list("n3_sb", n3)
+        cand_sb = load_list("cand_sb", cand)
+        tau_sb = load_rows("tau_sb", tau)
+        gs_sb = load_rows("gs_sb", gs)
+        n1_sb = load_list("n1_sb", n1)
+        n2_sb = load_list("n2_sb", n2)
+        gn_sb = load_rows("gn_sb", gn)
+        tau2_sb = load_rows("tau2_sb", tau2)
+        n5_sb = load_list("n5_sb", n5)
+        w2w_raw = load_fp4_words("w2w_raw", w2_words)
+        load_scale_rows(w2s_raw, w2_scales)
+        n6_sb = load_list("n6_sb", n6)
+
+        y = [window("y%d" % t, "y%d" % t) for t in range(PACK)]
+        b = [window("b%d" % t, "b%d" % t) for t in range(PACK)]
+
+        xq_scales = sb.tile([P, S], U8, name="xq_scales", align_bytes=64)
+        nc.vector.tensor_copy(xq_scales[:], xs_all[:].indirect(offs_sb[:]))
+        w1w = deal(nc.scalar.copy, "w1w", w1w_raw, U8, U16)
+        w1s = deal(nc.vector.tensor_copy, "w1s", w1s_raw, U8, U8)
+        xq_words = sb.tile([P, S], U32, name="xq_words", tag="picked_words", align_bytes=64)
+        nc.vector.tensor_copy(xq_words[:], xw_all[:].bitcast(U32).indirect(offs_sb[:]))
+
+        neg_tau = sb.tile([P, PACK], F32, name="neg_tau")
+        nc.scalar.activation(neg_tau[:], tau_sb[:], ACT.Copy, scale=-1.0)
+        neg_tau2 = sb.tile([P, PACK], F32, name="neg_tau2")
+        nc.scalar.activation(neg_tau2[:], tau2_sb[:], ACT.Copy, scale=-1.0)
+
+        top = sb.tile([P, PACK], F32, name="top")
+        for t in range(PACK):
+            bank = psum.tile([P, S], F32, name="y_bank%d" % t, tag="ya_bank%d" % t)
+            product(bank, fp4_block(w1w, t), w1s[:, P * t : P * (t + 1)], xq_words, xq_scales, 1)
+            nc.vector.tensor_scalar(
+                y[t][:, :S], bank[:], 1.0, None, op0=ALU.mult, op1=ALU.max, accum_out=top[:, t : t + 1]
+            )
+        bias = sb.tile([P, PACK], F32, name="bias")
+        nc.vector.tensor_tensor(bias[:], top[:], neg_tau[:], ALU.mult)
+
+        y4 = planes("y4")
+        gap = planes("gap")
+        th = planes("th")
+        half_gs_y = planes("half_gs_y")
+        z2 = planes("z2", BF16)
+        for t in range(PACK):
+            nc.scalar.activation(y4[:, t, :], y[t][:].indirect(n4_sb[:]), ACT.Copy)
+        for t in range(PACK):
+            nc.vector.tensor_tensor(gap[:, t, :], y[t][:].indirect(n3_sb[:]), y4[:, t, :], ALU.subtract)
+        for t in range(PACK):
+            nc.scalar.activation(th[:, t, :], gap[:, t, :], ACT.Tanh, scale=0.5)
+        for t in range(PACK):
+            nc.vector.tensor_scalar(
+                half_gs_y[:, t, :], y[t][:, :S], gs_sb[:, t : t + 1], 0.5, op0=ALU.mult, op1=ALU.mult
+            )
+        for t in range(PACK):
+            nc.vector.scalar_tensor_tensor(
+                z2[:, t, :], th[:, t, :], 1.0, half_gs_y[:, t, :], op0=ALU.add, op1=ALU.mult
+            )
+        z2_codes, z2_scales = quantise("z2", z2)
+
+        xc_scales_raw = sb.tile([P, C], U8, name="xc_scales_raw", align_bytes=64)
+        nc.vector.tensor_copy(xc_scales_raw[:], xs_all[:].indirect(cand_sb[:]))
+        xc_scales = deal(nc.vector.tensor_copy, "xc_scales", xc_scales_raw, U8, U8)
+        xc_words_raw = sb.tile([P, C], U32, name="xc_words_raw", tag="picked_words", align_bytes=64)
+        nc.vector.tensor_copy(xc_words_raw[:], xw_all[:].bitcast(U32).indirect(cand_sb[:]))
+        xc_words = deal(nc.vector.tensor_copy, "xc_words", xc_words_raw, I32, I32)
+
+        top2 = sb.tile([P, PACK], F32, name="top2")
+        bias2 = sb.tile([P, PACK], F32, name="bias2")
+        for t in range(PACK):
+            bank = psum.tile([P, S], F32, name="b_bank%d" % t)
+            rows = slice(P * t, P * (t + 1))
+            product(bank, xc_words[:, rows].bitcast(FP8X4), xc_scales[:, rows], z2_codes, z2_scales, 2)
+            nc.vector.tensor_scalar(
+                b[t][:, :S], bank[:], 0.0625, None, op0=ALU.mult, op1=ALU.max, accum_out=top2[:, t : t + 1]
+            )
+            nc.vector.tensor_tensor(bias2[:, t : t + 1], top2[:, t : t + 1], neg_tau2[:, t : t + 1], ALU.mult)
+
+        ea = planes("ea")
+        ea2 = planes("ea2")
+        ea_sum = planes("ea_sum")
+        gn_y = planes("gn_y")
+        for t in range(PACK):
+            rate, shift = tau_sb[:, t : t + 1], bias[:, t : t + 1]
+            nc.scalar.activation(ea[:, t, :], y[t][:].indirect(n1_sb[:]), ACT.Exp, bias=shift, scale=rate)
+            nc.scalar.activation(ea2[:, t, :], y[t][:].indirect(n2_sb[:]), ACT.Exp, bias=shift, scale=rate)
+        ea3 = planes("ea3")
+        for t in range(PACK):
+            nc.scalar.activation(
+                ea3[:, t, :], b[t][:].indirect(n5_sb[:]), ACT.Exp,
+                bias=bias2[:, t : t + 1], scale=tau2_sb[:, t : t + 1],
+            )
+        for t in range(PACK):
+            nc.vector.tensor_tensor(ea_sum[:, t, :], ea[:, t, :], ea2[:, t, :], ALU.add)
+            nc.vector.tensor_scalar(gn_y[:, t, :], y[t][:, :S], gn_sb[:, t : t + 1], None, op0=ALU.mult)
+        w2w = deal(nc.scalar.copy, "w2w", w2w_raw, U8, U16)
+        w2s = deal(nc.vector.tensor_copy, "w2s", w2s_raw, U8, U8)
+
+        log_sum = sb.tile([P, PACK, S], F32, name="log_sum", tag="b%d" % (PACK - 1))
+        z = planes("z", BF16)
+        for t in range(PACK):
+            nc.scalar.activation(log_sum[:, t, :], ea_sum[:, t, :], ACT.Ln, bias=0.25)
+            nc.vector.scalar_tensor_tensor(
+                z[:, t, :], log_sum[:, t, :], gn_sb[:, t : t + 1], gn_y[:, t, :], op0=ALU.mult, op1=ALU.add
+            )
+        log_den = planes("log_den")
+        nc.scalar.activation(log_den[:], ea3[:], ACT.Ln, bias=0.25)
+        z_codes, z_scales = quantise("z", z)
+        a = planes("a")
+        for t in range(PACK):
+            bank = psum.tile([P, S], F32, name="a_bank%d" % t, tag="ya_bank%d" % t)
+            product(bank, fp4_block(w2w, t), w2s[:, P * t : P * (t + 1)], z_codes, z_scales, 2)
+            nc.vector.tensor_copy(a[:, t, :], bank[:])
+
+        out_rows = out_0.rearrange("(p t) j -> p t j", t=PACK)
+        out_words = out_1[0].rearrange("p j t -> p (j t)").bitcast(I32)
+        o_codes = sb.tile([P, S], U32, name="o_codes", align_bytes=64)
+        o_scales = sb.tile([P, S], U8, name="o_scales", align_bytes=64)
+        for first, width in OUT_CHUNKS:
+            cols = slice(first, first + width)
+            shape = [P, PACK, width]
+            a6 = sb.tile(shape, F32, name="a6_%d" % first)
+            for t in range(PACK):
+                nc.scalar.activation(
+                    a6[:, t, :], a[:, t, :].indirect(n6_sb[:, first // 16 : (first + width) // 16]), ACT.Copy
+                )
+            inv_den = sb.tile(shape, F32, name="inv_den_%d" % first)
+            nc.scalar.activation(inv_den[:], log_den[:, :, cols], ACT.Exp, scale=-1.0)
+            diff = sb.tile(shape, F32, name="diff_%d" % first)
+            nc.vector.tensor_tensor(diff[:], a[:, :, cols], a6[:], ALU.subtract)
+            res = sb.tile(shape, F32, name="res_%d" % first)
+            nc.vector.scalar_tensor_tensor(res[:], diff[:], 0.5, inv_den[:], op0=ALU.mult, op1=ALU.mult)
+            nc.sync.dma_start(out_rows[:, :, cols], res[:])
+            woven = sb.tile([P, width, PACK], BF16, name="o_woven_%d" % first, align_bytes=64)
+            interleave(woven[:], res[:])
+            nc.vector.quantize_mx(
+                out=o_codes[:, cols].bitcast(FP8X4), scales=o_scales[:, cols],
+                in_=woven[:].rearrange("p j t -> p (j t)"),
+            )
+            nc.sync.dma_start(out_words[:, cols], o_codes[:, cols].bitcast(I32))
+        for q in range(4):
+            nc.sync.dma_start(out_2[0, 4 * q : 4 * q + 4, :].bitcast(I32), o_scales[32 * q : 32 * q + 4, :].bitcast(I32))

@@ -19,7 +19,6 @@ ACT = mybir.ActivationFunctionType
 P = 128
 PACK = 4
 HALF = S // 2
-OUT_CHUNKS = ((0, 256), (256, 128), (384, 128))
 
 
 def tile_picked_fkcdqxbelgcmp_none_po_kernel(
@@ -55,8 +54,8 @@ def tile_picked_fkcdqxbelgcmp_none_po_kernel(
             nc.sync.dma_start(tile[:].bitcast(I32), dram[0].bitcast(I32))
             return tile
 
-        def deal(engine_copy, name, src, dtype, view):
-            tile = sb.tile(list(src.shape), dtype, name=name, align_bytes=64)
+        def deal(engine_copy, name, src, dtype, view, tag=None):
+            tile = sb.tile(list(src.shape), dtype, name=name, tag=tag or name, align_bytes=64)
             engine_copy(
                 tile[:].bitcast(view).rearrange("p (t m) -> p t m", t=PACK),
                 src[:].bitcast(view).rearrange("p (m t) -> p t m", t=PACK),
@@ -71,8 +70,8 @@ def tile_picked_fkcdqxbelgcmp_none_po_kernel(
         def planes(name, dtype=F32, tag=None):
             return sb.tile([P, PACK, S], dtype, name=name, tag=tag or name, align_bytes=64)
 
-        def interleave(dst, src):
-            nc.vector.tensor_copy(
+        def interleave(engine_copy, dst, src):
+            engine_copy(
                 dst.rearrange("p (c i) t -> p c t i", i=4), src.rearrange("p t (c i) -> p c t i", i=4)
             )
 
@@ -82,7 +81,7 @@ def tile_picked_fkcdqxbelgcmp_none_po_kernel(
             scales = sb.tile([P, S], U8, name=name + "_scales", align_bytes=64)
             halves = [slice(h * HALF, (h + 1) * HALF) for h in range(2)]
             for cols in halves:
-                interleave(woven[:, cols, :], planar[:, :, cols])
+                interleave(nc.vector.tensor_copy, woven[:, cols, :], planar[:, :, cols])
             for cols in halves:
                 nc.vector.quantize_mx(
                     out=codes[:, cols].bitcast(FP8X4), scales=scales[:, cols],
@@ -106,14 +105,15 @@ def tile_picked_fkcdqxbelgcmp_none_po_kernel(
         w1s_raw = zeroed_bytes("w1s_raw", H, nc.gpsimd)
         w2s_raw = zeroed_bytes("w2s_raw", N, nc.gpsimd)
         offs_sb = load_list("offs_sb", offs)
-        w1w_raw = load_fp4_words("w1w_raw", w1_words)
+        cand_sb = load_list("cand_sb", cand)
         load_scale_rows(xs_all, x_scales)
         xw_all = sb.tile([P, T], I32, name="xw_all", align_bytes=64)
         nc.sync.dma_start(xw_all[:], x_words[0].rearrange("p n t -> p (n t)").bitcast(I32))
         load_scale_rows(w1s_raw, w1_scales)
+        w1w_raw = load_fp4_words("w1w_raw", w1_words)
         n4_sb = load_list("n4_sb", n4)
+        w2w_raw = load_fp4_words("w2w_raw", w2_words)
         n3_sb = load_list("n3_sb", n3)
-        cand_sb = load_list("cand_sb", cand)
         tau_sb = load_rows("tau_sb", tau)
         gs_sb = load_rows("gs_sb", gs)
         n1_sb = load_list("n1_sb", n1)
@@ -121,34 +121,35 @@ def tile_picked_fkcdqxbelgcmp_none_po_kernel(
         gn_sb = load_rows("gn_sb", gn)
         tau2_sb = load_rows("tau2_sb", tau2)
         n5_sb = load_list("n5_sb", n5)
-        w2w_raw = load_fp4_words("w2w_raw", w2_words)
         load_scale_rows(w2s_raw, w2_scales)
         n6_sb = load_list("n6_sb", n6)
 
         y = [window("y%d" % t, "y%d" % t) for t in range(PACK)]
-        b = [window("b%d" % t, "b%d" % t) for t in range(PACK)]
 
         xq_scales = sb.tile([P, S], U8, name="xq_scales", align_bytes=64)
         nc.vector.tensor_copy(xq_scales[:], xs_all[:].indirect(offs_sb[:]))
         w1w = deal(nc.scalar.copy, "w1w", w1w_raw, U8, U16)
-        w1s = deal(nc.vector.tensor_copy, "w1s", w1s_raw, U8, U8)
-        xq_words = sb.tile([P, S], U32, name="xq_words", tag="picked_words", align_bytes=64)
+        xq_words = sb.tile([P, S], U32, name="xq_words", align_bytes=64)
         nc.vector.tensor_copy(xq_words[:], xw_all[:].bitcast(U32).indirect(offs_sb[:]))
-
-        neg_tau = sb.tile([P, PACK], F32, name="neg_tau")
-        nc.scalar.activation(neg_tau[:], tau_sb[:], ACT.Copy, scale=-1.0)
-        neg_tau2 = sb.tile([P, PACK], F32, name="neg_tau2")
-        nc.scalar.activation(neg_tau2[:], tau2_sb[:], ACT.Copy, scale=-1.0)
+        w1s = deal(nc.vector.tensor_copy, "w1s", w1s_raw, U8, U8)
+        xc_words_raw = sb.tile([P, C], U32, name="xc_words_raw", tag="w1s_raw", align_bytes=64)
+        nc.vector.tensor_copy(xc_words_raw[:], xw_all[:].bitcast(U32).indirect(cand_sb[:]))
+        xc_scales_raw = sb.tile([P, C], U8, name="xc_scales_raw", align_bytes=64)
+        nc.vector.tensor_copy(xc_scales_raw[:], xs_all[:].indirect(cand_sb[:]))
 
         top = sb.tile([P, PACK], F32, name="top")
         for t in range(PACK):
             bank = psum.tile([P, S], F32, name="y_bank%d" % t, tag="ya_bank%d" % t)
             product(bank, fp4_block(w1w, t), w1s[:, P * t : P * (t + 1)], xq_words, xq_scales, 1)
-            nc.vector.tensor_scalar(
-                y[t][:, :S], bank[:], 1.0, None, op0=ALU.mult, op1=ALU.max, accum_out=top[:, t : t + 1]
-            )
+            if t == 0:
+                nc.scalar.copy(y[t][:, :S], bank[:])
+            else:
+                nc.vector.tensor_scalar(
+                    y[t][:, :S], bank[:], 1.0, None, op0=ALU.mult, op1=ALU.max, accum_out=top[:, t : t + 1]
+                )
+        nc.vector.tensor_reduce(top[:, 0:1], y[0][:, :S], axis=mybir.AxisListType.X, op=ALU.max)
         bias = sb.tile([P, PACK], F32, name="bias")
-        nc.vector.tensor_tensor(bias[:], top[:], neg_tau[:], ALU.mult)
+        nc.vector.scalar_tensor_tensor(bias[:], top[:], -1.0, tau_sb[:], op0=ALU.mult, op1=ALU.mult)
 
         y4 = planes("y4")
         gap = planes("gap")
@@ -169,25 +170,10 @@ def tile_picked_fkcdqxbelgcmp_none_po_kernel(
             nc.vector.scalar_tensor_tensor(
                 z2[:, t, :], th[:, t, :], 1.0, half_gs_y[:, t, :], op0=ALU.add, op1=ALU.mult
             )
+
+        xc_scales = deal(nc.vector.tensor_copy, "xc_scales", xc_scales_raw, U8, U8, tag="xq_scales")
+        xc_words = deal(nc.vector.tensor_copy, "xc_words", xc_words_raw, I32, I32, tag="xq_words")
         z2_codes, z2_scales = quantise("z2", z2)
-
-        xc_scales_raw = sb.tile([P, C], U8, name="xc_scales_raw", align_bytes=64)
-        nc.vector.tensor_copy(xc_scales_raw[:], xs_all[:].indirect(cand_sb[:]))
-        xc_scales = deal(nc.vector.tensor_copy, "xc_scales", xc_scales_raw, U8, U8)
-        xc_words_raw = sb.tile([P, C], U32, name="xc_words_raw", tag="picked_words", align_bytes=64)
-        nc.vector.tensor_copy(xc_words_raw[:], xw_all[:].bitcast(U32).indirect(cand_sb[:]))
-        xc_words = deal(nc.vector.tensor_copy, "xc_words", xc_words_raw, I32, I32)
-
-        top2 = sb.tile([P, PACK], F32, name="top2")
-        bias2 = sb.tile([P, PACK], F32, name="bias2")
-        for t in range(PACK):
-            bank = psum.tile([P, S], F32, name="b_bank%d" % t)
-            rows = slice(P * t, P * (t + 1))
-            product(bank, xc_words[:, rows].bitcast(FP8X4), xc_scales[:, rows], z2_codes, z2_scales, 2)
-            nc.vector.tensor_scalar(
-                b[t][:, :S], bank[:], 0.0625, None, op0=ALU.mult, op1=ALU.max, accum_out=top2[:, t : t + 1]
-            )
-            nc.vector.tensor_tensor(bias2[:, t : t + 1], top2[:, t : t + 1], neg_tau2[:, t : t + 1], ALU.mult)
 
         ea = planes("ea")
         ea2 = planes("ea2")
@@ -197,6 +183,21 @@ def tile_picked_fkcdqxbelgcmp_none_po_kernel(
             rate, shift = tau_sb[:, t : t + 1], bias[:, t : t + 1]
             nc.scalar.activation(ea[:, t, :], y[t][:].indirect(n1_sb[:]), ACT.Exp, bias=shift, scale=rate)
             nc.scalar.activation(ea2[:, t, :], y[t][:].indirect(n2_sb[:]), ACT.Exp, bias=shift, scale=rate)
+        b = y
+        top2 = sb.tile([P, PACK], F32, name="top2")
+        bias2 = sb.tile([P, PACK], F32, name="bias2")
+        for t in range(PACK):
+            bank = psum.tile([P, S], F32, name="b_bank%d" % t)
+            rows = slice(P * t, P * (t + 1))
+            product(bank, xc_words[:, rows].bitcast(FP8X4), xc_scales[:, rows], z2_codes, z2_scales, 2 if t == 0 else 1)
+            nc.vector.tensor_scalar(gn_y[:, t, :], y[t][:, :S], gn_sb[:, t : t + 1], None, op0=ALU.mult)
+            nc.vector.tensor_scalar(
+                b[t][:, :S], bank[:], 0.0625, None, op0=ALU.mult, op1=ALU.max, accum_out=top2[:, t : t + 1]
+            )
+            nc.vector.tensor_scalar(
+                bias2[:, t : t + 1], top2[:, t : t + 1], tau2_sb[:, t : t + 1], -1.0, op0=ALU.mult, op1=ALU.mult
+            )
+
         ea3 = planes("ea3")
         for t in range(PACK):
             nc.scalar.activation(
@@ -205,11 +206,10 @@ def tile_picked_fkcdqxbelgcmp_none_po_kernel(
             )
         for t in range(PACK):
             nc.vector.tensor_tensor(ea_sum[:, t, :], ea[:, t, :], ea2[:, t, :], ALU.add)
-            nc.vector.tensor_scalar(gn_y[:, t, :], y[t][:, :S], gn_sb[:, t : t + 1], None, op0=ALU.mult)
         w2w = deal(nc.scalar.copy, "w2w", w2w_raw, U8, U16)
         w2s = deal(nc.vector.tensor_copy, "w2s", w2s_raw, U8, U8)
 
-        log_sum = sb.tile([P, PACK, S], F32, name="log_sum", tag="b%d" % (PACK - 1))
+        log_sum = sb.tile([P, PACK, S], F32, name="log_sum", tag="y%d" % (PACK - 1))
         z = planes("z", BF16)
         for t in range(PACK):
             nc.scalar.activation(log_sum[:, t, :], ea_sum[:, t, :], ACT.Ln, bias=0.25)
@@ -222,34 +222,41 @@ def tile_picked_fkcdqxbelgcmp_none_po_kernel(
         a = planes("a")
         for t in range(PACK):
             bank = psum.tile([P, S], F32, name="a_bank%d" % t, tag="ya_bank%d" % t)
-            product(bank, fp4_block(w2w, t), w2s[:, P * t : P * (t + 1)], z_codes, z_scales, 2)
+            product(bank, fp4_block(w2w, t), w2s[:, P * t : P * (t + 1)], z_codes, z_scales, 2 if t == 0 else 1)
             nc.vector.tensor_copy(a[:, t, :], bank[:])
 
         out_rows = out_0.rearrange("(p t) j -> p t j", t=PACK)
         out_words = out_1[0].rearrange("p j t -> p (j t)").bitcast(I32)
         o_codes = sb.tile([P, S], U32, name="o_codes", align_bytes=64)
         o_scales = sb.tile([P, S], U8, name="o_scales", align_bytes=64)
-        for first, width in OUT_CHUNKS:
+        a6 = sb.tile([P, PACK, HALF], F32, name="a6")
+        inv_den = sb.tile([P, PACK, HALF], F32, name="inv_den")
+        diff = planes("diff")
+        res = planes("res")
+        chunks = ((0,256),(256,256))
+        for first, width in chunks:
             cols = slice(first, first + width)
-            shape = [P, PACK, width]
-            a6 = sb.tile(shape, F32, name="a6_%d" % first)
+            held = slice(first % HALF, first % HALF + width)
             for t in range(PACK):
+                nc.scalar.activation(inv_den[:, t, held], log_den[:, t, cols], ACT.Exp, scale=-1.0)
                 nc.scalar.activation(
-                    a6[:, t, :], a[:, t, :].indirect(n6_sb[:, first // 16 : (first + width) // 16]), ACT.Copy
+                    a6[:, t, held], a[:, t, :].indirect(n6_sb[:, first // 16 : (first + width) // 16]), ACT.Copy
                 )
-            inv_den = sb.tile(shape, F32, name="inv_den_%d" % first)
-            nc.scalar.activation(inv_den[:], log_den[:, :, cols], ACT.Exp, scale=-1.0)
-            diff = sb.tile(shape, F32, name="diff_%d" % first)
-            nc.vector.tensor_tensor(diff[:], a[:, :, cols], a6[:], ALU.subtract)
-            res = sb.tile(shape, F32, name="res_%d" % first)
-            nc.vector.scalar_tensor_tensor(res[:], diff[:], 0.5, inv_den[:], op0=ALU.mult, op1=ALU.mult)
-            nc.sync.dma_start(out_rows[:, :, cols], res[:])
-            woven = sb.tile([P, width, PACK], BF16, name="o_woven_%d" % first, align_bytes=64)
-            interleave(woven[:], res[:])
+                nc.vector.tensor_tensor(diff[:, t, cols], a[:, t, cols], a6[:, t, held], ALU.subtract)
+                nc.vector.scalar_tensor_tensor(
+                    res[:, t, cols], diff[:, t, cols], 0.5, inv_den[:, t, held], op0=ALU.mult, op1=ALU.mult
+                )
+            nc.sync.dma_start(out_rows[:, :, cols], res[:, :, cols])
+        woven = sb.tile([P, S, PACK], BF16, name="o_woven", align_bytes=64)
+        for first, width, engine_copy in ((0,256,nc.scalar.copy),(256,128,nc.vector.tensor_copy),(384,128,nc.vector.tensor_copy)):
+            cols = slice(first, first + width)
+            interleave(engine_copy, woven[:, cols, :], res[:, :, cols])
+        for first, width in ((0,384),(384,128)):
+            cols = slice(first, first + width)
             nc.vector.quantize_mx(
-                out=o_codes[:, cols].bitcast(FP8X4), scales=o_scales[:, cols],
-                in_=woven[:].rearrange("p j t -> p (j t)"),
+                out=o_codes[:, cols].bitcast(FP8X4), scales=o_scales[:, cols], in_=woven[:, cols, :].rearrange("p j t -> p (j t)")
             )
             nc.sync.dma_start(out_words[:, cols], o_codes[:, cols].bitcast(I32))
         for q in range(4):
-            nc.sync.dma_start(out_2[0, 4 * q : 4 * q + 4, :].bitcast(I32), o_scales[32 * q : 32 * q + 4, :].bitcast(I32))
+            queue = nc.scalar if q % 2 == 0 else nc.sync
+            queue.dma_start(out_2[0, 4 * q : 4 * q + 4, :].bitcast(I32), o_scales[32 * q : 32 * q + 4, :].bitcast(I32))

@@ -19,6 +19,7 @@ ACT = mybir.ActivationFunctionType
 P = 128
 PACK = 4
 HALF = S // 2
+EXACT = 384
 
 
 def tile_picked_fkcdqxbelgcmp_none_po_kernel(
@@ -131,7 +132,12 @@ def tile_picked_fkcdqxbelgcmp_none_po_kernel(
         w1w = deal(nc.scalar.copy, "w1w", w1w_raw, U8, U16)
         xq_words = sb.tile([P, S], U32, name="xq_words", align_bytes=64)
         nc.vector.tensor_copy(xq_words[:], xw_all[:].bitcast(U32).indirect(offs_sb[:]))
-        w1s = deal(nc.vector.tensor_copy, "w1s", w1s_raw, U8, U8)
+        w1s = sb.tile([P, H], U8, name="w1s", align_bytes=64)
+        for ts in (slice(0, 1), slice(1, PACK)):
+            nc.vector.tensor_copy(
+                w1s[:].rearrange("p (t m) -> p t m", t=PACK)[:, ts, :],
+                w1s_raw[:].rearrange("p (m t) -> p t m", t=PACK)[:, ts, :],
+            )
         xc_words_raw = sb.tile([P, C], U32, name="xc_words_raw", tag="w1s_raw", align_bytes=64)
         nc.vector.tensor_copy(xc_words_raw[:], xw_all[:].bitcast(U32).indirect(cand_sb[:]))
         xc_scales_raw = sb.tile([P, C], U8, name="xc_scales_raw", align_bytes=64)
@@ -155,6 +161,8 @@ def tile_picked_fkcdqxbelgcmp_none_po_kernel(
         gap = planes("gap")
         th = planes("th")
         half_gs_y = planes("half_gs_y")
+        half_gs = sb.tile([P, PACK], F32, name="half_gs")
+        nc.gpsimd.tensor_scalar(half_gs[:], gs_sb[:], 0.5, 0.0, op0=ALU.mult, op1=ALU.add)
         z2 = planes("z2", BF16)
         for t in range(PACK):
             nc.scalar.activation(y4[:, t, :], y[t][:].indirect(n4_sb[:]), ACT.Copy)
@@ -163,8 +171,8 @@ def tile_picked_fkcdqxbelgcmp_none_po_kernel(
         for t in range(PACK):
             nc.scalar.activation(th[:, t, :], gap[:, t, :], ACT.Tanh, scale=0.5)
         for t in range(PACK):
-            nc.vector.tensor_scalar(
-                half_gs_y[:, t, :], y[t][:, :S], gs_sb[:, t : t + 1], 0.5, op0=ALU.mult, op1=ALU.mult
+            nc.gpsimd.tensor_scalar(
+                half_gs_y[:, t, :], y[t][:, :S], half_gs[:, t : t + 1], 0.0, op0=ALU.mult, op1=ALU.add
             )
         for t in range(PACK):
             nc.vector.scalar_tensor_tensor(
@@ -206,18 +214,27 @@ def tile_picked_fkcdqxbelgcmp_none_po_kernel(
             )
         for t in range(PACK):
             nc.vector.tensor_tensor(ea_sum[:, t, :], ea[:, t, :], ea2[:, t, :], ALU.add)
+        den_first = sb.tile([P, EXACT], F32, name="den_first")
+        inv_first = sb.tile([P, S], F32, name="inv_first")
+        nc.vector.tensor_scalar(den_first[:], ea3[:, 0, :EXACT], 0.25, None, op0=ALU.add)
         w2w = deal(nc.scalar.copy, "w2w", w2w_raw, U8, U16)
         w2s = deal(nc.vector.tensor_copy, "w2s", w2s_raw, U8, U8)
+        nc.vector.reciprocal(inv_first[:, :EXACT], den_first[:])
 
         log_sum = sb.tile([P, PACK, S], F32, name="log_sum", tag="y%d" % (PACK - 1))
         z = planes("z", BF16)
         for t in range(PACK):
             nc.scalar.activation(log_sum[:, t, :], ea_sum[:, t, :], ACT.Ln, bias=0.25)
-            nc.vector.scalar_tensor_tensor(
-                z[:, t, :], log_sum[:, t, :], gn_sb[:, t : t + 1], gn_y[:, t, :], op0=ALU.mult, op1=ALU.add
-            )
+            for cols in [slice(0, S)] if t < PACK - 1 else [slice(0, HALF), slice(HALF, S)]:
+                nc.vector.scalar_tensor_tensor(
+                    z[:, t, cols], log_sum[:, t, cols], gn_sb[:, t : t + 1], gn_y[:, t, cols], op0=ALU.mult, op1=ALU.add
+                )
         log_den = planes("log_den")
-        nc.scalar.activation(log_den[:], ea3[:], ACT.Ln, bias=0.25)
+        nc.scalar.activation(
+            log_den[:].rearrange("p t j -> p (t j)")[:, EXACT:], ea3[:].rearrange("p t j -> p (t j)")[:, EXACT:],
+            ACT.Ln, bias=0.25,
+        )
+        nc.scalar.activation(inv_first[:, EXACT:], log_den[:, 0, EXACT:], ACT.Exp, scale=-1.0)
         z_codes, z_scales = quantise("z", z)
         a = planes("a")
         for t in range(PACK):
@@ -238,13 +255,17 @@ def tile_picked_fkcdqxbelgcmp_none_po_kernel(
             cols = slice(first, first + width)
             held = slice(first % HALF, first % HALF + width)
             for t in range(PACK):
-                nc.scalar.activation(inv_den[:, t, held], log_den[:, t, cols], ACT.Exp, scale=-1.0)
+                if t == 0:
+                    inverse = inv_first[:, cols]
+                else:
+                    inverse = inv_den[:, t, held]
+                    nc.scalar.activation(inverse, log_den[:, t, cols], ACT.Exp, scale=-1.0)
                 nc.scalar.activation(
                     a6[:, t, held], a[:, t, :].indirect(n6_sb[:, first // 16 : (first + width) // 16]), ACT.Copy
                 )
                 nc.vector.tensor_tensor(diff[:, t, cols], a[:, t, cols], a6[:, t, held], ALU.subtract)
                 nc.vector.scalar_tensor_tensor(
-                    res[:, t, cols], diff[:, t, cols], 0.5, inv_den[:, t, held], op0=ALU.mult, op1=ALU.mult
+                    res[:, t, cols], diff[:, t, cols], 0.5, inverse, op0=ALU.mult, op1=ALU.mult
                 )
             nc.sync.dma_start(out_rows[:, :, cols], res[:, :, cols])
         woven = sb.tile([P, S, PACK], BF16, name="o_woven", align_bytes=64)

@@ -19,7 +19,7 @@ ACT = mybir.ActivationFunctionType
 P = 128
 PACK = 4
 HALF = S // 2
-EXACT = 384
+EXACT = S
 
 
 def tile_picked_fkcdqxbelgcmp_none_po_kernel(
@@ -112,8 +112,8 @@ def tile_picked_fkcdqxbelgcmp_none_po_kernel(
         nc.sync.dma_start(xw_all[:], x_words[0].rearrange("p n t -> p (n t)").bitcast(I32))
         load_scale_rows(w1s_raw, w1_scales)
         w1w_raw = load_fp4_words("w1w_raw", w1_words)
-        n4_sb = load_list("n4_sb", n4)
         w2w_raw = load_fp4_words("w2w_raw", w2_words)
+        n4_sb = load_list("n4_sb", n4)
         n3_sb = load_list("n3_sb", n3)
         tau_sb = load_rows("tau_sb", tau)
         gs_sb = load_rows("gs_sb", gs)
@@ -129,11 +129,19 @@ def tile_picked_fkcdqxbelgcmp_none_po_kernel(
 
         xq_scales = sb.tile([P, S], U8, name="xq_scales", align_bytes=64)
         nc.vector.tensor_copy(xq_scales[:], xs_all[:].indirect(offs_sb[:]))
-        w1w = deal(nc.scalar.copy, "w1w", w1w_raw, U8, U16)
-        xq_words = sb.tile([P, S], U32, name="xq_words", align_bytes=64)
-        nc.vector.tensor_copy(xq_words[:], xw_all[:].bitcast(U32).indirect(offs_sb[:]))
-        w1s = sb.tile([P, H], U8, name="w1s", align_bytes=64)
+        w1w = sb.tile([P, 2 * H], U8, name="w1w", align_bytes=64)
         for ts in (slice(0, 1), slice(1, PACK)):
+            nc.scalar.copy(
+                w1w[:].bitcast(U16).rearrange("p (t m) -> p t m", t=PACK)[:, ts, :],
+                w1w_raw[:].bitcast(U16).rearrange("p (m t) -> p t m", t=PACK)[:, ts, :],
+            )
+        xq_words = sb.tile([P, S], U32, name="xq_words", align_bytes=64)
+        w1s = sb.tile([P, H], U8, name="w1s", align_bytes=64)
+        for h, ts in enumerate((slice(0, 1), slice(1, PACK))):
+            nc.vector.tensor_copy(
+                xq_words[:, h * HALF : (h + 1) * HALF],
+                xw_all[:].bitcast(U32).indirect(offs_sb[:, h * HALF // 16 : (h + 1) * HALF // 16]),
+            )
             nc.vector.tensor_copy(
                 w1s[:].rearrange("p (t m) -> p t m", t=PACK)[:, ts, :],
                 w1s_raw[:].rearrange("p (m t) -> p t m", t=PACK)[:, ts, :],
@@ -144,15 +152,20 @@ def tile_picked_fkcdqxbelgcmp_none_po_kernel(
         nc.vector.tensor_copy(xc_scales_raw[:], xs_all[:].indirect(cand_sb[:]))
 
         top = sb.tile([P, PACK], F32, name="top")
-        for t in range(PACK):
+        for h in range(2):
+            cols = slice(h * HALF, (h + 1) * HALF)
+            bank = psum.tile([P, HALF], F32, name="y_half_bank%d" % h, tag="b_bank%d" % h)
+            nc.tensor.matmul_mx(
+                out=bank[:], lhsT=fp4_block(w1w, 0), lhsT_scale=w1s[:, :P],
+                rhs=xq_words[:, cols].bitcast(FP8X4), rhs_scale=xq_scales[:, cols], start=True, stop=True,
+            )
+            nc.scalar.copy(y[0][:, cols], bank[:])
+        for t in range(1, PACK):
             bank = psum.tile([P, S], F32, name="y_bank%d" % t, tag="ya_bank%d" % t)
             product(bank, fp4_block(w1w, t), w1s[:, P * t : P * (t + 1)], xq_words, xq_scales, 1)
-            if t == 0:
-                nc.scalar.copy(y[t][:, :S], bank[:])
-            else:
-                nc.vector.tensor_scalar(
-                    y[t][:, :S], bank[:], 1.0, None, op0=ALU.mult, op1=ALU.max, accum_out=top[:, t : t + 1]
-                )
+            nc.vector.tensor_scalar(
+                y[t][:, :S], bank[:], 1.0, None, op0=ALU.mult, op1=ALU.max, accum_out=top[:, t : t + 1]
+            )
         nc.vector.tensor_reduce(top[:, 0:1], y[0][:, :S], axis=mybir.AxisListType.X, op=ALU.max)
         bias = sb.tile([P, PACK], F32, name="bias")
         nc.vector.scalar_tensor_tensor(bias[:], top[:], -1.0, tau_sb[:], op0=ALU.mult, op1=ALU.mult)
@@ -168,6 +181,15 @@ def tile_picked_fkcdqxbelgcmp_none_po_kernel(
             nc.scalar.activation(y4[:, t, :], y[t][:].indirect(n4_sb[:]), ACT.Copy)
         for t in range(PACK):
             nc.vector.tensor_tensor(gap[:, t, :], y[t][:].indirect(n3_sb[:]), y4[:, t, :], ALU.subtract)
+        ea = planes("ea")
+        ea2 = planes("ea2")
+
+        def fetch_exponentials(t):
+            rate, shift = tau_sb[:, t : t + 1], bias[:, t : t + 1]
+            nc.scalar.activation(ea[:, t, :], y[t][:].indirect(n1_sb[:]), ACT.Exp, bias=shift, scale=rate)
+            nc.scalar.activation(ea2[:, t, :], y[t][:].indirect(n2_sb[:]), ACT.Exp, bias=shift, scale=rate)
+
+        fetch_exponentials(0)
         for t in range(PACK):
             nc.scalar.activation(th[:, t, :], gap[:, t, :], ACT.Tanh, scale=0.5)
         for t in range(PACK):
@@ -183,14 +205,10 @@ def tile_picked_fkcdqxbelgcmp_none_po_kernel(
         xc_words = deal(nc.vector.tensor_copy, "xc_words", xc_words_raw, I32, I32, tag="xq_words")
         z2_codes, z2_scales = quantise("z2", z2)
 
-        ea = planes("ea")
-        ea2 = planes("ea2")
         ea_sum = planes("ea_sum")
         gn_y = planes("gn_y")
-        for t in range(PACK):
-            rate, shift = tau_sb[:, t : t + 1], bias[:, t : t + 1]
-            nc.scalar.activation(ea[:, t, :], y[t][:].indirect(n1_sb[:]), ACT.Exp, bias=shift, scale=rate)
-            nc.scalar.activation(ea2[:, t, :], y[t][:].indirect(n2_sb[:]), ACT.Exp, bias=shift, scale=rate)
+        for t in range(1, PACK):
+            fetch_exponentials(t)
         b = y
         top2 = sb.tile([P, PACK], F32, name="top2")
         bias2 = sb.tile([P, PACK], F32, name="bias2")
@@ -199,10 +217,12 @@ def tile_picked_fkcdqxbelgcmp_none_po_kernel(
             rows = slice(P * t, P * (t + 1))
             product(bank, xc_words[:, rows].bitcast(FP8X4), xc_scales[:, rows], z2_codes, z2_scales, 2 if t == 0 else 1)
             nc.vector.tensor_scalar(gn_y[:, t, :], y[t][:, :S], gn_sb[:, t : t + 1], None, op0=ALU.mult)
+            if t > 0:
+                nc.vector.tensor_tensor(ea_sum[:, t - 1, :], ea[:, t - 1, :], ea2[:, t - 1, :], ALU.add)
             nc.vector.tensor_scalar(
                 b[t][:, :S], bank[:], 0.0625, None, op0=ALU.mult, op1=ALU.max, accum_out=top2[:, t : t + 1]
             )
-            nc.vector.tensor_scalar(
+            nc.gpsimd.tensor_scalar(
                 bias2[:, t : t + 1], top2[:, t : t + 1], tau2_sb[:, t : t + 1], -1.0, op0=ALU.mult, op1=ALU.mult
             )
 
@@ -212,8 +232,7 @@ def tile_picked_fkcdqxbelgcmp_none_po_kernel(
                 ea3[:, t, :], b[t][:].indirect(n5_sb[:]), ACT.Exp,
                 bias=bias2[:, t : t + 1], scale=tau2_sb[:, t : t + 1],
             )
-        for t in range(PACK):
-            nc.vector.tensor_tensor(ea_sum[:, t, :], ea[:, t, :], ea2[:, t, :], ALU.add)
+        nc.vector.tensor_tensor(ea_sum[:, PACK - 1, :], ea[:, PACK - 1, :], ea2[:, PACK - 1, :], ALU.add)
         den_first = sb.tile([P, EXACT], F32, name="den_first")
         inv_first = sb.tile([P, S], F32, name="inv_first")
         nc.vector.tensor_scalar(den_first[:], ea3[:, 0, :EXACT], 0.25, None, op0=ALU.add)
@@ -234,7 +253,6 @@ def tile_picked_fkcdqxbelgcmp_none_po_kernel(
             log_den[:].rearrange("p t j -> p (t j)")[:, EXACT:], ea3[:].rearrange("p t j -> p (t j)")[:, EXACT:],
             ACT.Ln, bias=0.25,
         )
-        nc.scalar.activation(inv_first[:, EXACT:], log_den[:, 0, EXACT:], ACT.Exp, scale=-1.0)
         z_codes, z_scales = quantise("z", z)
         a = planes("a")
         for t in range(PACK):

from contextlib import ExitStack

import concourse.mybir as mybir

K, T, S, N, H, C = 512, 2048, 512, 512, 512, 512
FLOPS = 2 * K * H * S + 2 * H * N * S + 2 * K * C * S

F32 = mybir.dt.float32
BF16 = mybir.dt.bfloat16
I32 = mybir.dt.int32
U32 = mybir.dt.uint32
U16 = mybir.dt.uint16
U8 = mybir.dt.uint8
FP8X4 = mybir.dt.float8_e4m3fn_x4
FP4X4 = mybir.dt.float4_e2m1fn_x4
ALU = mybir.AluOpType
ACT = mybir.ActivationFunctionType

P = 128
PACK = 4
HALF = S // 2
EXACT = S


def tile_picked_fkcdqxbelgcmp_none_po_kernel(
    tc, x_words, x_scales, w1_words, w1_scales, tau, gn, w2_words, w2_scales, gs, tau2,
    offs, n1, n2, n3, n4, cand, n5, n6, out_0, out_1, out_2,
):
    nc = tc.nc
    with ExitStack() as ctx:
        sb = ctx.enter_context(tc.tile_pool(name="sb", bufs=1))
        psum = ctx.enter_context(tc.psum_pool(name="psum", bufs=1))

        def load_list(name, dram):
            tile = sb.tile([P, S // 16], U16, name=name)
            nc.sync.dma_start(tile[:], dram)
            return tile

        def load_rows(name, dram):
            tile = sb.tile([P, PACK], F32, name=name)
            nc.sync.dma_start(tile[:], dram.rearrange("(p t) o -> p (t o)", t=PACK))
            return tile

        def load_scale_rows(tile, dram):
            for q in range(4):
                nc.sync.dma_start(tile[32 * q : 32 * q + 4, :].bitcast(I32), dram[0, 4 * q : 4 * q + 4, :].bitcast(I32))

        def zeroed_bytes(name, width, engine):
            tile = sb.tile([P, width], U8, name=name, align_bytes=64)
            engine.memset(tile[:].bitcast(I32), 0)
            return tile

        def load_fp4_words(name, dram):
            tile = sb.tile([P, 2 * H], U8, name=name, align_bytes=64)
            nc.sync.dma_start(tile[:].bitcast(I32), dram[0].bitcast(I32))
            return tile

        def deal(engine_copy, name, src, dtype, view, tag=None):
            tile = sb.tile(list(src.shape), dtype, name=name, tag=tag or name, align_bytes=64)
            engine_copy(
                tile[:].bitcast(view).rearrange("p (t m) -> p t m", t=PACK),
                src[:].bitcast(view).rearrange("p (m t) -> p t m", t=PACK),
            )
            return tile

        def window(name, tag):
            tile = sb.tile([P, 2 * S], F32, name=name, tag=tag)
            nc.vector.memset(tile[:, S:], 0.0)
            return tile

        def planes(name, dtype=F32, tag=None):
            return sb.tile([P, PACK, S], dtype, name=name, tag=tag or name, align_bytes=64)

        def interleave(engine_copy, dst, src):
            engine_copy(
                dst.rearrange("p (c i) t -> p c t i", i=4), src.rearrange("p t (c i) -> p c t i", i=4)
            )

        def quantise(name, planar):
            woven = sb.tile([P, S, PACK], BF16, name=name + "_woven", align_bytes=64)
            codes = sb.tile([P, S], U32, name=name + "_codes", align_bytes=64)
            scales = sb.tile([P, S], U8, name=name + "_scales", align_bytes=64)
            halves = [slice(h * HALF, (h + 1) * HALF) for h in range(2)]
            for cols in halves:
                interleave(nc.vector.tensor_copy, woven[:, cols, :], planar[:, :, cols])
            for cols in halves:
                nc.vector.quantize_mx(
                    out=codes[:, cols].bitcast(FP8X4), scales=scales[:, cols],
                    in_=woven[:, cols, :].rearrange("p j t -> p (j t)"),
                )
            return codes, scales

        def product(bank, lhs, lhs_scales, codes, scales, pieces):
            width = S // pieces
            for h in range(pieces):
                cols = slice(h * width, (h + 1) * width)
                nc.tensor.matmul_mx(
                    out=bank[:, cols], lhsT=lhs, lhsT_scale=lhs_scales,
                    rhs=codes[:, cols].bitcast(FP8X4), rhs_scale=scales[:, cols], start=True, stop=True,
                )

        def fp4_block(words, t):
            return words[:, 2 * P * t : 2 * P * (t + 1)].bitcast(FP4X4)

        xs_all = zeroed_bytes("xs_all", T, nc.vector)
        w1s_raw = zeroed_bytes("w1s_raw", H, nc.gpsimd)
        w2s_raw = zeroed_bytes("w2s_raw", N, nc.gpsimd)
        offs_sb = load_list("offs_sb", offs)
        cand_sb = load_list("cand_sb", cand)
        load_scale_rows(xs_all, x_scales)
        xw_all = sb.tile([P, T], I32, name="xw_all", align_bytes=64)
        nc.sync.dma_start(xw_all[:], x_words[0].rearrange("p n t -> p (n t)").bitcast(I32))
        load_scale_rows(w1s_raw, w1_scales)
        w1w_raw = load_fp4_words("w1w_raw", w1_words)
        w2w_raw = load_fp4_words("w2w_raw", w2_words)
        n4_sb = load_list("n4_sb", n4)
        n3_sb = load_list("n3_sb", n3)
        tau_sb = load_rows("tau_sb", tau)
        gs_sb = load_rows("gs_sb", gs)
        n1_sb = load_list("n1_sb", n1)
        n2_sb = load_list("n2_sb", n2)
        gn_sb = load_rows("gn_sb", gn)
        tau2_sb = load_rows("tau2_sb", tau2)
        n5_sb = load_list("n5_sb", n5)
        load_scale_rows(w2s_raw, w2_scales)
        n6_sb = load_list("n6_sb", n6)

        y = [window("y%d" % t, "y%d" % t) for t in range(PACK)]

        xq_scales = sb.tile([P, S], U8, name="xq_scales", align_bytes=64)
        nc.vector.tensor_copy(xq_scales[:], xs_all[:].indirect(offs_sb[:]))
        w1w = sb.tile([P, 2 * H], U8, name="w1w", align_bytes=64)
        for ts in (slice(0, 1), slice(1, PACK)):
            nc.scalar.copy(
                w1w[:].bitcast(U16).rearrange("p (t m) -> p t m", t=PACK)[:, ts, :],
                w1w_raw[:].bitcast(U16).rearrange("p (m t) -> p t m", t=PACK)[:, ts, :],
            )
        xq_words = sb.tile([P, S], U32, name="xq_words", align_bytes=64)
        w1s = sb.tile([P, H], U8, name="w1s", align_bytes=64)
        for h, ts in enumerate((slice(0, 1), slice(1, PACK))):
            nc.vector.tensor_copy(
                xq_words[:, h * HALF : (h + 1) * HALF],
                xw_all[:].bitcast(U32).indirect(offs_sb[:, h * HALF // 16 : (h + 1) * HALF // 16]),
            )
            nc.vector.tensor_copy(
                w1s[:].rearrange("p (t m) -> p t m", t=PACK)[:, ts, :],
                w1s_raw[:].rearrange("p (m t) -> p t m", t=PACK)[:, ts, :],
            )
        xc_words_raw = sb.tile([P, C], U32, name="xc_words_raw", tag="w1s_raw", align_bytes=64)
        nc.vector.tensor_copy(xc_words_raw[:], xw_all[:].bitcast(U32).indirect(cand_sb[:]))
        xc_scales_raw = sb.tile([P, C], U8, name="xc_scales_raw", align_bytes=64)
        nc.vector.tensor_copy(xc_scales_raw[:], xs_all[:].indirect(cand_sb[:]))

        top = sb.tile([P, PACK], F32, name="top")
        for h in range(2):
            cols = slice(h * HALF, (h + 1) * HALF)
            bank = psum.tile([P, HALF], F32, name="y_half_bank%d" % h, tag="b_bank%d" % h)
            nc.tensor.matmul_mx(
                out=bank[:], lhsT=fp4_block(w1w, 0), lhsT_scale=w1s[:, :P],
                rhs=xq_words[:, cols].bitcast(FP8X4), rhs_scale=xq_scales[:, cols], start=True, stop=True,
            )
            nc.scalar.copy(y[0][:, cols], bank[:])
        for t in range(1, PACK):
            bank = psum.tile([P, S], F32, name="y_bank%d" % t, tag="ya_bank%d" % t)
            product(bank, fp4_block(w1w, t), w1s[:, P * t : P * (t + 1)], xq_words, xq_scales, 1)
            nc.vector.tensor_scalar(
                y[t][:, :S], bank[:], 1.0, None, op0=ALU.mult, op1=ALU.max, accum_out=top[:, t : t + 1]
            )
        nc.vector.tensor_reduce(top[:, 0:1], y[0][:, :S], axis=mybir.AxisListType.X, op=ALU.max)
        bias = sb.tile([P, PACK], F32, name="bias")
        nc.vector.scalar_tensor_tensor(bias[:], top[:], -1.0, tau_sb[:], op0=ALU.mult, op1=ALU.mult)

        y4 = planes("y4")
        gap = planes("gap")
        th = planes("th")
        half_gs_y = planes("half_gs_y")
        half_gs = sb.tile([P, PACK], F32, name="half_gs")
        nc.gpsimd.tensor_scalar(half_gs[:], gs_sb[:], 0.5, 0.0, op0=ALU.mult, op1=ALU.add)
        z2 = planes("z2", BF16)
        for t in range(PACK):
            nc.scalar.activation(y4[:, t, :], y[t][:].indirect(n4_sb[:]), ACT.Copy)
        for t in range(PACK):
            nc.vector.tensor_tensor(gap[:, t, :], y[t][:].indirect(n3_sb[:]), y4[:, t, :], ALU.subtract)
        ea = planes("ea")
        ea2 = planes("ea2")

        def fetch_exponentials(t):
            rate, shift = tau_sb[:, t : t + 1], bias[:, t : t + 1]
            nc.scalar.activation(ea[:, t, :], y[t][:].indirect(n1_sb[:]), ACT.Exp, bias=shift, scale=rate)
            nc.scalar.activation(ea2[:, t, :], y[t][:].indirect(n2_sb[:]), ACT.Exp, bias=shift, scale=rate)

        fetch_exponentials(0)
        for t in range(PACK):
            nc.scalar.activation(th[:, t, :], gap[:, t, :], ACT.Tanh, scale=0.5)
        for t in range(PACK):
            nc.gpsimd.tensor_scalar(
                half_gs_y[:, t, :], y[t][:, :S], half_gs[:, t : t + 1], 0.0, op0=ALU.mult, op1=ALU.add
            )
        for t in range(PACK):
            nc.vector.scalar_tensor_tensor(
                z2[:, t, :], th[:, t, :], 1.0, half_gs_y[:, t, :], op0=ALU.add, op1=ALU.mult
            )

        xc_scales = deal(nc.vector.tensor_copy, "xc_scales", xc_scales_raw, U8, U8, tag="xq_scales")
        xc_words = deal(nc.vector.tensor_copy, "xc_words", xc_words_raw, I32, I32, tag="xq_words")
        z2_codes, z2_scales = quantise("z2", z2)

        ea_sum = planes("ea_sum")
        gn_y = planes("gn_y")
        for t in range(1, PACK):
            fetch_exponentials(t)
        b = y
        top2 = sb.tile([P, PACK], F32, name="top2")
        bias2 = sb.tile([P, PACK], F32, name="bias2")
        for t in range(PACK):
            bank = psum.tile([P, S], F32, name="b_bank%d" % t)
            rows = slice(P * t, P * (t + 1))
            product(bank, xc_words[:, rows].bitcast(FP8X4), xc_scales[:, rows], z2_codes, z2_scales, 2 if t == 0 else 1)
            nc.vector.tensor_scalar(gn_y[:, t, :], y[t][:, :S], gn_sb[:, t : t + 1], None, op0=ALU.mult)
            if t > 0:
                nc.vector.tensor_tensor(ea_sum[:, t - 1, :], ea[:, t - 1, :], ea2[:, t - 1, :], ALU.add)
            nc.vector.tensor_scalar(
                b[t][:, :S], bank[:], 0.0625, None, op0=ALU.mult, op1=ALU.max, accum_out=top2[:, t : t + 1]
            )
            nc.gpsimd.tensor_scalar(
                bias2[:, t : t + 1], top2[:, t : t + 1], tau2_sb[:, t : t + 1], -1.0, op0=ALU.mult, op1=ALU.mult
            )

        ea3 = planes("ea3")
        for t in range(PACK):
            nc.scalar.activation(
                ea3[:, t, :], b[t][:].indirect(n5_sb[:]), ACT.Exp,
                bias=bias2[:, t : t + 1], scale=tau2_sb[:, t : t + 1],
            )
        nc.vector.tensor_tensor(ea_sum[:, PACK - 1, :], ea[:, PACK - 1, :], ea2[:, PACK - 1, :], ALU.add)
        den_first = sb.tile([P, EXACT], F32, name="den_first")
        inv_first = sb.tile([P, S], F32, name="inv_first")
        nc.vector.tensor_scalar(den_first[:], ea3[:, 0, :EXACT], 0.25, None, op0=ALU.add)
        w2w = deal(nc.scalar.copy, "w2w", w2w_raw, U8, U16)
        w2s = deal(nc.vector.tensor_copy, "w2s", w2s_raw, U8, U8)
        nc.vector.reciprocal(inv_first[:, :EXACT], den_first[:])

        log_sum = sb.tile([P, PACK, S], F32, name="log_sum", tag="y%d" % (PACK - 1))
        z = planes("z", BF16)
        for t in range(PACK):
            nc.scalar.activation(log_sum[:, t, :], ea_sum[:, t, :], ACT.Ln, bias=0.25)
            for cols in [slice(0, S)] if t < PACK - 1 else [slice(0, HALF), slice(HALF, S)]:
                nc.vector.scalar_tensor_tensor(
                    z[:, t, cols], log_sum[:, t, cols], gn_sb[:, t : t + 1], gn_y[:, t, cols], op0=ALU.mult, op1=ALU.add
                )
        log_den = planes("log_den")
        nc.scalar.activation(
            log_den[:].rearrange("p t j -> p (t j)")[:, EXACT:], ea3[:].rearrange("p t j -> p (t j)")[:, EXACT:],
            ACT.Ln, bias=0.25,
        )
        z_codes, z_scales = quantise("z", z)
        a = planes("a")
        for t in range(PACK):
            bank = psum.tile([P, S], F32, name="a_bank%d" % t, tag="ya_bank%d" % t)
            product(bank, fp4_block(w2w, t), w2s[:, P * t : P * (t + 1)], z_codes, z_scales, 2 if t == 0 else 1)
            nc.vector.tensor_copy(a[:, t, :], bank[:])

        out_rows = out_0.rearrange("(p t) j -> p t j", t=PACK)
        out_words = out_1[0].rearrange("p j t -> p (j t)").bitcast(I32)
        o_codes = sb.tile([P, S], U32, name="o_codes", align_bytes=64)
        o_scales = sb.tile([P, S], U8, name="o_scales", align_bytes=64)
        a6 = sb.tile([P, PACK, HALF], F32, name="a6")
        inv_den = sb.tile([P, PACK, HALF], F32, name="inv_den")
        diff = planes("diff")
        res = planes("res")
        chunks = ((0,256),(256,256))
        for first, width in chunks:
            cols = slice(first, first + width)
            held = slice(first % HALF, first % HALF + width)
            for t in range(PACK):
                if t == 0:
                    inverse = inv_first[:, cols]
                else:
                    inverse = inv_den[:, t, held]
                    nc.scalar.activation(inverse, log_den[:, t, cols], ACT.Exp, scale=-1.0)
                nc.scalar.activation(
                    a6[:, t, held], a[:, t, :].indirect(n6_sb[:, first // 16 : (first + width) // 16]), ACT.Copy
                )
                nc.vector.tensor_tensor(diff[:, t, cols], a[:, t, cols], a6[:, t, held], ALU.subtract)
                nc.vector.scalar_tensor_tensor(
                    res[:, t, cols], diff[:, t, cols], 0.5, inverse, op0=ALU.mult, op1=ALU.mult
                )
            nc.sync.dma_start(out_rows[:, :, cols], res[:, :, cols])
        woven = sb.tile([P, S, PACK], BF16, name="o_woven", align_bytes=64)
        for first, width, engine_copy in ((0,256,nc.scalar.copy),(256,128,nc.vector.tensor_copy),(384,128,nc.vector.tensor_copy)):
            cols = slice(first, first + width)
            interleave(engine_copy, woven[:, cols, :], res[:, :, cols])
        for first, width in ((0,384),(384,128)):
            cols = slice(first, first + width)
            nc.vector.quantize_mx(
                out=o_codes[:, cols].bitcast(FP8X4), scales=o_scales[:, cols], in_=woven[:, cols, :].rearrange("p j t -> p (j t)")
            )
            nc.sync.dma_start(out_words[:, cols], o_codes[:, cols].bitcast(I32))
        for q in range(4):
            queue = nc.scalar if q % 2 == 0 else nc.sync
            queue.dma_start(out_2[0, 4 * q : 4 * q + 4, :].bitcast(I32), o_scales[32 * q : 32 * q + 4, :].bitcast(I32))
